import numpy as np
import ml_dtypes


def mxq(x, axis, fmt="e4m3"):
    dtype, down = {"e4m3": (ml_dtypes.float8_e4m3fn, 7), "e5m2": (ml_dtypes.float8_e5m2, 14)}[fmt]
    v = np.moveaxis(np.asarray(x, np.float32).astype(ml_dtypes.bfloat16).astype(np.float64), axis, -1)
    blocks = v.reshape(v.shape[:-1] + (-1, 32))
    amax = np.abs(blocks).max(-1, keepdims=True)
    byte = np.maximum(np.where(amax > 0, np.frexp(amax)[1] - 1 + 127, 0) - down, 1)
    scale = np.exp2(byte - 127.0)
    codes = (blocks / scale).astype(np.float32).astype(dtype).astype(np.float64)
    return np.moveaxis((codes * scale).reshape(v.shape), -1, axis)


WIDE = False


def mx_kscale(k):
    if not WIDE:
        return np.ones(k)
    levels = np.array([10, -10, 5, -5, 0])
    if k % 512:
        return np.exp2(np.random.permutation(np.resize(levels, k // 32))).repeat(32)
    a = np.empty((k // 512, 16))
    for p in range(k // 512):
        a[p, :8] = np.random.permutation(np.resize(levels, 8))
        for g in range(8):
            far = levels[np.abs(levels - a[p, g]) >= 10]
            a[p, g + 8] = far[np.random.randint(len(far))]
    return np.exp2(a.ravel()).repeat(32)


def f64(x):
    return np.asarray(x).astype(np.float64)


def striped8(idx):
    return np.concatenate([x.reshape(-1, 16).T for x in idx]).astype(np.uint16)


def runs(offs, k):
    lists = np.stack([offs[16 * r : 16 * r + 16].T.reshape(-1) for r in range(8)]).astype(np.int64)
    return lists[np.arange(k) % 512 // 64]


def pack_weight(w):
    k, n = w.shape
    w = f64(np.asarray(w, np.float32).astype(ml_dtypes.bfloat16)).reshape(k // 32, 32, n)
    amax = np.abs(w).max(1)
    byte = np.clip(np.where(amax > 0, np.frexp(amax)[1] - 1 + 127 - 7, 1), 1, 254)
    scaled = (w * np.exp2(127.0 - byte)[:, None, :]).reshape(k, n).astype(np.float32)
    words = np.ascontiguousarray(scaled.reshape(k // 512, 128, 4, n).transpose(0, 1, 3, 2)).astype(ml_dtypes.float8_e4m3fn).view(np.uint8)
    return words, np.ascontiguousarray(byte.astype(np.uint8).reshape(k // 512, 16, n))


def unpack_weight(words, scales):
    g, p, n, _ = words.shape
    vals = np.ascontiguousarray(words).view(ml_dtypes.float8_e4m3fn).astype(np.float64) * np.repeat(np.exp2(scales.astype(np.float64) - 127.0), 8, axis=1)[..., None]
    return vals.transpose(0, 1, 3, 2).reshape(g * 512, n)


def sigmoid(v):
    return 1.0 / (1.0 + np.exp(-np.maximum(v, -700.0)))

def planes(y):
    n, m = y.shape
    v = y.astype(np.float32).astype(ml_dtypes.bfloat16).astype(np.float64).reshape(n // 32, 32, m)
    top = np.abs(v).max(1)
    byte = np.clip(np.where(top > 0, np.frexp(top)[1] - 1 + 127 - 7, 1), 1, 254)
    codes = (v * np.exp2(127.0 - byte)[:, None, :]).reshape(n, m).astype(np.float32).astype(ml_dtypes.float8_e4m3fn).view(np.uint8)
    words = codes.reshape(n // 512, 128, 4, m).transpose(0, 1, 3, 2)
    return np.ascontiguousarray(words), np.ascontiguousarray(byte.astype(np.uint8).reshape(n // 512, 16, m))


K, T, S, N = 512, 2048, 512, 512


def setup_inputs():
    n = np.random.standard_normal
    s = mx_kscale(K)[:, None]
    packed_xT = pack_weight(n((K, T)) * s)
    return {
        "x_words": packed_xT[0],
        "x_scales": packed_xT[1],
        "hid": n((N, S)).astype(np.float32),
        "w1": (n((K, N)) / np.sqrt(K) / s).astype(np.float32),
        "w2": (n((K, N)) / np.sqrt(K) / s).astype(np.float32),
        "offs": striped8(np.random.randint(0, T, (8, S))),
    }


def reference(x_words, x_scales, hid, w1, w2, offs):
    xq = unpack_weight(x_words, x_scales)[np.arange(K)[:, None], runs(offs, K)]
    s = sigmoid(f64(hid) * ((mxq(f64(w1), 0, "e4m3").T @ xq)))
    val = mxq(f64(w2), 0, "e4m3").T @ xq
    out_0 = f64(hid) + s * val
    return (out_0,) + planes(out_0)

@@ -1,0 +1,167 @@
+from contextlib import ExitStack
+
+import concourse.mybir as mybir
+
+K, T, S, N = 512, 2048, 512, 512
+FLOPS = 2 * 2 * K * N * S
+
+F32 = mybir.dt.float32
+BF16 = mybir.dt.bfloat16
+I32 = mybir.dt.int32
+U32 = mybir.dt.uint32
+U16 = mybir.dt.uint16
+U8 = mybir.dt.uint8
+FP8X4 = mybir.dt.float8_e4m3fn_x4
+MULT = mybir.AluOpType.mult
+ADD = mybir.AluOpType.add
+SIGMOID = mybir.ActivationFunctionType.Sigmoid
+
+P = 128
+PACK = 4
+CHUNK = 128
+CHUNKS = S // CHUNK
+HALF = 256
+
+
+def tile_picked_engramh_none_po_kernel(
+    tc, x_words, x_scales, hid, w1, w2, offs, out_0, out_1, out_2
+):
+    nc = tc.nc
+    with ExitStack() as ctx:
+        keep = ctx.enter_context(tc.tile_pool(name="keep", bufs=1))
+        psum = ctx.enter_context(tc.psum_pool(name="psum", bufs=1))
+
+        offsets = keep.tile([P, S // 16], U16, name="offsets")
+        nc.sync.dma_start(offsets[:], offs)
+
+        scale_table = keep.tile([P, T], U8, name="scale_table", align_bytes=64)
+        nc.vector.memset(scale_table[:].bitcast(I32), 0)
+        nc.scalar.dma_start(scale_table[0:P:8, :].bitcast(I32), x_scales[0].bitcast(I32))
+        x_plane = keep.tile([P, S], U8, name="x_plane", align_bytes=64)
+        nc.vector.memset(x_plane[:].bitcast(I32), 0)
+
+        warm_in = keep.tile([P, 1], F32, name="warm_in")
+        warm_out = keep.tile([P, 1], F32, name="warm_out")
+        nc.vector.memset(warm_in[:], 0.0)
+        nc.scalar.activation(warm_out[:], warm_in[:], SIGMOID)
+
+        w1_raw = keep.tile([P, PACK, N], F32, name="w1_raw")
+        nc.sync.dma_start(w1_raw[:], w1.rearrange("(p j) c -> p j c", j=PACK))
+        word_table = keep.tile([P, T], I32, name="word_table", align_bytes=64)
+        nc.sync.dma_start(word_table[:], x_words[0].rearrange("p n t -> p (n t)").bitcast(I32))
+        w2_raw = []
+        for h in range(2):
+            part = keep.tile([P, PACK, HALF], F32, name="w2_raw%d" % h)
+            nc.sync.dma_start(part[:], w2.rearrange("(p j) c -> p j c", j=PACK)[:, :, h * HALF : (h + 1) * HALF])
+            w2_raw.append(part)
+        hid_rows = hid.rearrange("(p t) j -> p t j", t=PACK)
+        hid_half = []
+        for h in range(2):
+            part = keep.tile([P, PACK, HALF], F32, name="hid%d" % h)
+            nc.sync.dma_start(part[:], hid_rows[:, :, h * HALF : (h + 1) * HALF])
+            hid_half.append(part)
+
+        picked_scales = keep.tile([P, S], U8, name="picked_scales", align_bytes=64)
+        nc.vector.tensor_copy(picked_scales[:], scale_table[:].indirect(offsets[:]))
+        for r in range(4):
+            nc.scalar.dma_start(x_plane[r:P:32, :].bitcast(I32), picked_scales[8 * r : P : 32, :].bitcast(I32))
+
+        def deal(engine_copy, grouped, raw, m0, lo, hi):
+            engine_copy(
+                grouped[:].rearrange("p (t m j) -> p m j t", t=PACK, j=PACK)[:, lo:hi],
+                raw[:].rearrange("p j (m t) -> p m j t", t=PACK)[:, lo - m0 : hi - m0],
+            )
+
+        def quantize(grouped, label):
+            codes = keep.tile([P, N], U32, name=label + "_codes", align_bytes=64)
+            plane = keep.tile([P, N], U8, name=label + "_plane", align_bytes=64)
+            nc.vector.quantize_mx(out=codes[:].bitcast(FP8X4), scales=plane[:], in_=grouped[:])
+            return codes, plane
+
+        w1_grouped = keep.tile([P, PACK * N], BF16, name="w1_grouped", align_bytes=64)
+        deal(nc.vector.tensor_copy, w1_grouped, w1_raw, 0, 0, P)
+        w1_codes, w1_plane = quantize(w1_grouped, "w1")
+
+        x_codes = keep.tile([P, S], U32, name="x_codes", align_bytes=64)
+        nc.vector.tensor_copy(x_codes[:], word_table[:].bitcast(U32).indirect(offsets[:]))
+
+        def product(codes, plane, c, label):
+            bank = psum.tile([P, PACK, CHUNK], F32, name="%s%d" % (label, c))
+            cols = slice(c * CHUNK, (c + 1) * CHUNK)
+            for t in range(PACK):
+                nc.tensor.matmul_mx(
+                    out=bank[:, t, :],
+                    lhsT=codes[:, t * P : (t + 1) * P].bitcast(FP8X4),
+                    lhsT_scale=plane[:, t * P : (t + 1) * P],
+                    rhs=x_codes[:, cols].bitcast(FP8X4),
+                    rhs_scale=x_plane[:, cols],
+                    start=True,
+                    stop=True,
+                )
+            return bank
+
+        keys = [product(w1_codes, w1_plane, c, "key") for c in range(CHUNKS)]
+
+        w2_grouped = keep.tile([P, PACK * N], BF16, name="w2_grouped", align_bytes=64)
+        deal(nc.scalar.copy, w2_grouped, w2_raw[0], 0, 0, 64)
+        deal(nc.scalar.copy, w2_grouped, w2_raw[1], 64, 64, 84)
+        deal(nc.vector.tensor_copy, w2_grouped, w2_raw[1], 64, 84, P)
+        w2_codes, w2_plane = quantize(w2_grouped, "w2")
+        vals = [product(w2_codes, w2_plane, c, "val") for c in range(CHUNKS)]
+
+        out_rows = out_0.rearrange("(p t) j -> p t j", t=PACK)
+        y_codes = keep.tile([P, S], U32, name="y_codes", align_bytes=64)
+        y_plane = keep.tile([P, S], U8, name="y_plane", align_bytes=64)
+        out_words = out_1[0].rearrange("p n t -> p (n t)").bitcast(I32)
+
+        def hid_chunk(c):
+            lo = (c * CHUNK) % HALF
+            return hid_half[c * CHUNK // HALF][:, :, lo : lo + CHUNK]
+
+        gates, gated, results, grouped = {}, {}, {}, {}
+
+        def gate(c):
+            logits = keep.tile([P, PACK, CHUNK], F32, name="logits%d" % c)
+            nc.vector.tensor_tensor(logits[:], hid_chunk(c), keys[c][:], MULT)
+            gates[c] = keep.tile([P, PACK, CHUNK], F32, name="gate%d" % c)
+            nc.scalar.activation(gates[c][:], logits[:], SIGMOID)
+
+        def weigh(c):
+            gated[c] = keep.tile([P, PACK, CHUNK], F32, name="gated%d" % c)
+            nc.vector.tensor_tensor(gated[c][:], gates[c][:], vals[c][:], MULT)
+
+        def finish(c, adder, rounder):
+            results[c] = keep.tile([P, PACK, CHUNK], F32, name="result%d" % c)
+            adder(results[c][:], hid_chunk(c), gated[c][:], ADD)
+            nc.sync.dma_start(out_rows[:, :, c * CHUNK : (c + 1) * CHUNK], results[c][:])
+            grouped[c] = keep.tile([P, PACK * CHUNK], BF16, name="y_grouped%d" % c, align_bytes=64)
+            rounder(
+                grouped[c][:].rearrange("p (c i t) -> p c t i", i=4, t=PACK),
+                results[c][:].rearrange("p t (c i) -> p c t i", i=4),
+            )
+
+        def pack(c):
+            cols = slice(c * CHUNK, (c + 1) * CHUNK)
+            nc.vector.quantize_mx(out=y_codes[:, cols].bitcast(FP8X4), scales=y_plane[:, cols], in_=grouped[c][:])
+
+        gate(0)
+        gate(1)
+        weigh(0)
+        finish(0, nc.gpsimd.tensor_tensor, nc.scalar.copy)
+        gate(2)
+        weigh(1)
+        finish(1, nc.gpsimd.tensor_tensor, nc.scalar.copy)
+        gate(3)
+        weigh(2)
+        finish(2, nc.gpsimd.tensor_tensor, nc.scalar.copy)
+        pack(0)
+        weigh(3)
+        pack(1)
+        finish(3, nc.vector.tensor_tensor, nc.vector.tensor_copy)
+        pack(2)
+        nc.sync.dma_start(out_words[:, 0 : 3 * CHUNK], y_codes[:, 0 : 3 * CHUNK].bitcast(I32))
+        pack(3)
+        nc.sync.dma_start(out_words[:, 3 * CHUNK : S], y_codes[:, 3 * CHUNK : S].bitcast(I32))
+        for q in range(4):
+            queue = nc.scalar if q % 2 == 0 else nc.sync
+            queue.dma_start(out_2[0, 4 * q : 4 * q + 4, :].bitcast(I32), y_plane[32 * q : 32 * q + 4, :].bitcast(I32))

@@ -36,7 +36,6 @@ def tile_picked_engramh_none_po_kernel(
 
         scale_table = keep.tile([P, T], U8, name="scale_table", align_bytes=64)
         nc.vector.memset(scale_table[:].bitcast(I32), 0)
-        nc.scalar.dma_start(scale_table[0:P:8, :].bitcast(I32), x_scales[0].bitcast(I32))
         x_plane = keep.tile([P, S], U8, name="x_plane", align_bytes=64)
         nc.vector.memset(x_plane[:].bitcast(I32), 0)
 
@@ -46,25 +45,26 @@ def tile_picked_engramh_none_po_kernel(
         nc.scalar.activation(warm_out[:], warm_in[:], SIGMOID)
 
         w1_raw = keep.tile([P, PACK, N], F32, name="w1_raw")
-        nc.sync.dma_start(w1_raw[:], w1.rearrange("(p j) c -> p j c", j=PACK))
+        w1_rows = w1.rearrange("(p j) c -> p j c", j=PACK)
+        nc.sync.dma_start(w1_raw[:, 0:2, :], w1_rows[:, 0:2, :])
+        nc.sync.dma_start(scale_table[0:P:8, :].bitcast(I32), x_scales[0].bitcast(I32))
+        nc.sync.dma_start(w1_raw[:, 2:4, :], w1_rows[:, 2:4, :])
+        w2_raw = keep.tile([P, PACK, N], F32, name="w2_raw")
+        nc.sync.dma_start(w2_raw[:], w2.rearrange("(p j) c -> p j c", j=PACK))
         word_table = keep.tile([P, T], I32, name="word_table", align_bytes=64)
         nc.sync.dma_start(word_table[:], x_words[0].rearrange("p n t -> p (n t)").bitcast(I32))
-        w2_raw = []
-        for h in range(2):
-            part = keep.tile([P, PACK, HALF], F32, name="w2_raw%d" % h)
-            nc.sync.dma_start(part[:], w2.rearrange("(p j) c -> p j c", j=PACK)[:, :, h * HALF : (h + 1) * HALF])
-            w2_raw.append(part)
+
+        picked_scales = keep.tile([P, S], U8, name="picked_scales", align_bytes=64)
+        nc.vector.tensor_copy(picked_scales[:], scale_table[:].indirect(offsets[:]))
+        for r in range(4):
+            nc.sync.dma_start(x_plane[r:P:32, :].bitcast(I32), picked_scales[8 * r : P : 32, :].bitcast(I32))
+
         hid_rows = hid.rearrange("(p t) j -> p t j", t=PACK)
         hid_half = []
         for h in range(2):
             part = keep.tile([P, PACK, HALF], F32, name="hid%d" % h)
             nc.sync.dma_start(part[:], hid_rows[:, :, h * HALF : (h + 1) * HALF])
             hid_half.append(part)
-
-        picked_scales = keep.tile([P, S], U8, name="picked_scales", align_bytes=64)
-        nc.vector.tensor_copy(picked_scales[:], scale_table[:].indirect(offsets[:]))
-        for r in range(4):
-            nc.scalar.dma_start(x_plane[r:P:32, :].bitcast(I32), picked_scales[8 * r : P : 32, :].bitcast(I32))
 
         def deal(engine_copy, grouped, raw, m0, lo, hi):
             engine_copy(
@@ -82,8 +82,17 @@ def tile_picked_engramh_none_po_kernel(
         deal(nc.vector.tensor_copy, w1_grouped, w1_raw, 0, 0, P)
         w1_codes, w1_plane = quantize(w1_grouped, "w1")
 
+        w2_grouped = keep.tile([P, PACK * N], BF16, name="w2_grouped", align_bytes=64)
+        deal(nc.scalar.copy, w2_grouped, w2_raw, 0, 0, 44)
+        deal(nc.vector.tensor_copy, w2_grouped, w2_raw, 0, 44, P)
+        w2_codes, w2_plane = quantize(w2_grouped, "w2")
+
         x_codes = keep.tile([P, S], U32, name="x_codes", align_bytes=64)
-        nc.vector.tensor_copy(x_codes[:], word_table[:].bitcast(U32).indirect(offsets[:]))
+        for h in range(2):
+            nc.vector.tensor_copy(
+                x_codes[:, h * HALF : (h + 1) * HALF],
+                word_table[:].bitcast(U32).indirect(offsets[:, h * HALF // 16 : (h + 1) * HALF // 16]),
+            )
 
         def product(codes, plane, c, label):
             bank = psum.tile([P, PACK, CHUNK], F32, name="%s%d" % (label, c))
@@ -100,14 +109,12 @@ def tile_picked_engramh_none_po_kernel(
                 )
             return bank
 
-        keys = [product(w1_codes, w1_plane, c, "key") for c in range(CHUNKS)]
-
-        w2_grouped = keep.tile([P, PACK * N], BF16, name="w2_grouped", align_bytes=64)
-        deal(nc.scalar.copy, w2_grouped, w2_raw[0], 0, 0, 64)
-        deal(nc.scalar.copy, w2_grouped, w2_raw[1], 64, 64, 84)
-        deal(nc.vector.tensor_copy, w2_grouped, w2_raw[1], 64, 84, P)
-        w2_codes, w2_plane = quantize(w2_grouped, "w2")
-        vals = [product(w2_codes, w2_plane, c, "val") for c in range(CHUNKS)]
+        keys, vals = {}, {}
+        for label, c in (("key", 0), ("key", 1), ("val", 0), ("key", 2), ("val", 1), ("key", 3), ("val", 2), ("val", 3)):
+            if label == "key":
+                keys[c] = product(w1_codes, w1_plane, c, label)
+            else:
+                vals[c] = product(w2_codes, w2_plane, c, label)
 
         out_rows = out_0.rearrange("(p t) j -> p t j", t=PACK)
         y_codes = keep.tile([P, S], U32, name="y_codes", align_bytes=64)
@@ -118,7 +125,8 @@ def tile_picked_engramh_none_po_kernel(
             lo = (c * CHUNK) % HALF
             return hid_half[c * CHUNK // HALF][:, :, lo : lo + CHUNK]
 
-        gates, gated, results, grouped = {}, {}, {}, {}
+        gates, gated, results = {}, {}, {}
+        grouped = [keep.tile([P, PACK * HALF], BF16, name="y_grouped%d" % h, align_bytes=64) for h in range(2)]
 
         def gate(c):
             logits = keep.tile([P, PACK, CHUNK], F32, name="logits%d" % c)
@@ -130,38 +138,50 @@ def tile_picked_engramh_none_po_kernel(
             gated[c] = keep.tile([P, PACK, CHUNK], F32, name="gated%d" % c)
             nc.vector.tensor_tensor(gated[c][:], gates[c][:], vals[c][:], MULT)
 
-        def finish(c, adder, rounder):
+        def finish(c, adder):
             results[c] = keep.tile([P, PACK, CHUNK], F32, name="result%d" % c)
             adder(results[c][:], hid_chunk(c), gated[c][:], ADD)
             nc.sync.dma_start(out_rows[:, :, c * CHUNK : (c + 1) * CHUNK], results[c][:])
-            grouped[c] = keep.tile([P, PACK * CHUNK], BF16, name="y_grouped%d" % c, align_bytes=64)
+
+        def weave(c, rounder, lo, hi):
+            base = (c * CHUNK) % HALF
             rounder(
-                grouped[c][:].rearrange("p (c i t) -> p c t i", i=4, t=PACK),
-                results[c][:].rearrange("p t (c i) -> p c t i", i=4),
+                grouped[c * CHUNK // HALF][:, PACK * (base + lo) : PACK * (base + hi)].rearrange(
+                    "p (c i t) -> p c t i", i=4, t=PACK
+                ),
+                results[c][:, :, lo:hi].rearrange("p t (c i) -> p c t i", i=4),
             )
 
-        def pack(c):
-            cols = slice(c * CHUNK, (c + 1) * CHUNK)
-            nc.vector.quantize_mx(out=y_codes[:, cols].bitcast(FP8X4), scales=y_plane[:, cols], in_=grouped[c][:])
+        def pack(lo, hi):
+            base = lo % HALF
+            nc.vector.quantize_mx(
+                out=y_codes[:, lo:hi].bitcast(FP8X4),
+                scales=y_plane[:, lo:hi],
+                in_=grouped[lo // HALF][:, PACK * base : PACK * (base + hi - lo)],
+            )
 
         gate(0)
         gate(1)
         weigh(0)
-        finish(0, nc.gpsimd.tensor_tensor, nc.scalar.copy)
+        finish(0, nc.gpsimd.tensor_tensor)
         gate(2)
         weigh(1)
-        finish(1, nc.gpsimd.tensor_tensor, nc.scalar.copy)
+        finish(1, nc.gpsimd.tensor_tensor)
         gate(3)
+        weave(0, nc.scalar.copy, 0, CHUNK)
         weigh(2)
-        finish(2, nc.gpsimd.tensor_tensor, nc.scalar.copy)
-        pack(0)
+        weave(1, nc.scalar.copy, 0, CHUNK)
         weigh(3)
-        pack(1)
-        finish(3, nc.vector.tensor_tensor, nc.vector.tensor_copy)
-        pack(2)
-        nc.sync.dma_start(out_words[:, 0 : 3 * CHUNK], y_codes[:, 0 : 3 * CHUNK].bitcast(I32))
-        pack(3)
-        nc.sync.dma_start(out_words[:, 3 * CHUNK : S], y_codes[:, 3 * CHUNK : S].bitcast(I32))
+        finish(2, nc.vector.tensor_tensor)
+        weave(2, nc.scalar.copy, 0, CHUNK)
+        finish(3, nc.vector.tensor_tensor)
+        weave(3, nc.scalar.copy, 0, 48)
+        pack(0, HALF)
+        nc.sync.dma_start(out_words[:, 0:HALF], y_codes[:, 0:HALF].bitcast(I32))
+        weave(3, nc.vector.tensor_copy, 48, CHUNK)
+        pack(2 * CHUNK, 3 * CHUNK)
+        pack(3 * CHUNK, S)
+        nc.sync.dma_start(out_words[:, HALF:S], y_codes[:, HALF:S].bitcast(I32))
         for q in range(4):
             queue = nc.scalar if q % 2 == 0 else nc.sync
             queue.dma_start(out_2[0, 4 * q : 4 * q + 4, :].bitcast(I32), y_plane[32 * q : 32 * q + 4, :].bitcast(I32))

@@ -49,16 +49,18 @@ def tile_picked_engramh_none_po_kernel(
         nc.sync.dma_start(w1_raw[:, 0:2, :], w1_rows[:, 0:2, :])
         nc.sync.dma_start(scale_table[0:P:8, :].bitcast(I32), x_scales[0].bitcast(I32))
         nc.sync.dma_start(w1_raw[:, 2:4, :], w1_rows[:, 2:4, :])
-        w2_raw = keep.tile([P, PACK, N], F32, name="w2_raw")
-        nc.sync.dma_start(w2_raw[:], w2.rearrange("(p j) c -> p j c", j=PACK))
         word_table = keep.tile([P, T], I32, name="word_table", align_bytes=64)
         nc.sync.dma_start(word_table[:], x_words[0].rearrange("p n t -> p (n t)").bitcast(I32))
+        w2_rows = w2.rearrange("(p j) c -> p j c", j=PACK)
+        w2_raw = [keep.tile([P, PACK, HALF], F32, name="w2_raw%d" % h) for h in range(2)]
+        nc.sync.dma_start(w2_raw[0][:], w2_rows[:, :, 0:HALF])
 
         picked_scales = keep.tile([P, S], U8, name="picked_scales", align_bytes=64)
         nc.vector.tensor_copy(picked_scales[:], scale_table[:].indirect(offsets[:]))
         for r in range(4):
             nc.sync.dma_start(x_plane[r:P:32, :].bitcast(I32), picked_scales[8 * r : P : 32, :].bitcast(I32))
 
+        nc.sync.dma_start(w2_raw[1][:], w2_rows[:, :, HALF:N])
         hid_rows = hid.rearrange("(p t) j -> p t j", t=PACK)
         hid_half = []
         for h in range(2):
@@ -68,8 +70,8 @@ def tile_picked_engramh_none_po_kernel(
 
         def deal(engine_copy, grouped, raw, m0, lo, hi):
             engine_copy(
-                grouped[:].rearrange("p (t m j) -> p m j t", t=PACK, j=PACK)[:, lo:hi],
-                raw[:].rearrange("p j (m t) -> p m j t", t=PACK)[:, lo - m0 : hi - m0],
+                grouped[:].rearrange("p (u v m j) -> p u m j v", u=2, v=2, j=PACK)[:, :, lo:hi],
+                raw[:].rearrange("p j (m u v) -> p u m j v", u=2, v=2)[:, :, lo - m0 : hi - m0],
             )
 
         def quantize(grouped, label):
@@ -79,20 +81,12 @@ def tile_picked_engramh_none_po_kernel(
             return codes, plane
 
         w1_grouped = keep.tile([P, PACK * N], BF16, name="w1_grouped", align_bytes=64)
-        deal(nc.vector.tensor_copy, w1_grouped, w1_raw, 0, 0, P)
+        deal(nc.scalar.copy, w1_grouped, w1_raw, 0, 0, 44)
+        deal(nc.vector.tensor_copy, w1_grouped, w1_raw, 0, 44, P)
         w1_codes, w1_plane = quantize(w1_grouped, "w1")
 
-        w2_grouped = keep.tile([P, PACK * N], BF16, name="w2_grouped", align_bytes=64)
-        deal(nc.scalar.copy, w2_grouped, w2_raw, 0, 0, 44)
-        deal(nc.vector.tensor_copy, w2_grouped, w2_raw, 0, 44, P)
-        w2_codes, w2_plane = quantize(w2_grouped, "w2")
-
         x_codes = keep.tile([P, S], U32, name="x_codes", align_bytes=64)
-        for h in range(2):
-            nc.vector.tensor_copy(
-                x_codes[:, h * HALF : (h + 1) * HALF],
-                word_table[:].bitcast(U32).indirect(offsets[:, h * HALF // 16 : (h + 1) * HALF // 16]),
-            )
+        nc.vector.tensor_copy(x_codes[:], word_table[:].bitcast(U32).indirect(offsets[:]))
 
         def product(codes, plane, c, label):
             bank = psum.tile([P, PACK, CHUNK], F32, name="%s%d" % (label, c))
@@ -109,12 +103,7 @@ def tile_picked_engramh_none_po_kernel(
                 )
             return bank
 
-        keys, vals = {}, {}
-        for label, c in (("key", 0), ("key", 1), ("val", 0), ("key", 2), ("val", 1), ("key", 3), ("val", 2), ("val", 3)):
-            if label == "key":
-                keys[c] = product(w1_codes, w1_plane, c, label)
-            else:
-                vals[c] = product(w2_codes, w2_plane, c, label)
+        keys = [product(w1_codes, w1_plane, c, "key") for c in range(CHUNKS)]
 
         out_rows = out_0.rearrange("(p t) j -> p t j", t=PACK)
         y_codes = keep.tile([P, S], U32, name="y_codes", align_bytes=64)
@@ -138,10 +127,18 @@ def tile_picked_engramh_none_po_kernel(
             gated[c] = keep.tile([P, PACK, CHUNK], F32, name="gated%d" % c)
             nc.vector.tensor_tensor(gated[c][:], gates[c][:], vals[c][:], MULT)
 
+        middle = keep.tile([P, PACK, HALF], F32, name="result12")
+        results[0] = keep.tile([P, PACK, CHUNK], F32, name="result0")[:]
+        results[1] = middle[:, :, 0:CHUNK]
+        results[2] = middle[:, :, CHUNK:HALF]
+        results[3] = keep.tile([P, PACK, CHUNK], F32, name="result3")[:]
+
         def finish(c, adder):
-            results[c] = keep.tile([P, PACK, CHUNK], F32, name="result%d" % c)
-            adder(results[c][:], hid_chunk(c), gated[c][:], ADD)
-            nc.sync.dma_start(out_rows[:, :, c * CHUNK : (c + 1) * CHUNK], results[c][:])
+            adder(results[c], hid_chunk(c), gated[c][:], ADD)
+            if c == 2:
+                nc.sync.dma_start(out_rows[:, :, CHUNK : 3 * CHUNK], middle[:])
+            elif c != 1:
+                nc.sync.dma_start(out_rows[:, :, c * CHUNK : (c + 1) * CHUNK], results[c])
 
         def weave(c, rounder, lo, hi):
             base = (c * CHUNK) % HALF
@@ -160,14 +157,22 @@ def tile_picked_engramh_none_po_kernel(
                 in_=grouped[lo // HALF][:, PACK * base : PACK * (base + hi - lo)],
             )
 
+        w2_grouped = keep.tile([P, PACK * N], BF16, name="w2_grouped", align_bytes=64)
+        deal(nc.scalar.copy, w2_grouped, w2_raw[0], 0, 0, 32)
+        deal(nc.vector.tensor_copy, w2_grouped, w2_raw[0], 0, 32, 64)
+        deal(nc.scalar.copy, w2_grouped, w2_raw[1], 64, 64, 84)
+        deal(nc.vector.tensor_copy, w2_grouped, w2_raw[1], 64, 84, P)
+        w2_codes, w2_plane = quantize(w2_grouped, "w2")
+        vals = [product(w2_codes, w2_plane, c, "val") for c in range(CHUNKS)]
+
         gate(0)
         gate(1)
         weigh(0)
         finish(0, nc.gpsimd.tensor_tensor)
         gate(2)
+        gate(3)
         weigh(1)
         finish(1, nc.gpsimd.tensor_tensor)
-        gate(3)
         weave(0, nc.scalar.copy, 0, CHUNK)
         weigh(2)
         weave(1, nc.scalar.copy, 0, CHUNK)

from contextlib import ExitStack

import concourse.mybir as mybir

K, T, S, N = 512, 2048, 512, 512
FLOPS = 2 * 2 * K * N * S

F32 = mybir.dt.float32
BF16 = mybir.dt.bfloat16
I32 = mybir.dt.int32
U32 = mybir.dt.uint32
U16 = mybir.dt.uint16
U8 = mybir.dt.uint8
FP8X4 = mybir.dt.float8_e4m3fn_x4
MULT = mybir.AluOpType.mult
ADD = mybir.AluOpType.add
SIGMOID = mybir.ActivationFunctionType.Sigmoid

P = 128
PACK = 4
CHUNK = 128
CHUNKS = S // CHUNK
HALF = 256


def tile_picked_engramh_none_po_kernel(
    tc, x_words, x_scales, hid, w1, w2, offs, out_0, out_1, out_2
):
    nc = tc.nc
    with ExitStack() as ctx:
        keep = ctx.enter_context(tc.tile_pool(name="keep", bufs=1))
        psum = ctx.enter_context(tc.psum_pool(name="psum", bufs=1))

        offsets = keep.tile([P, S // 16], U16, name="offsets")
        nc.sync.dma_start(offsets[:], offs)

        scale_table = keep.tile([P, T], U8, name="scale_table", align_bytes=64)
        nc.vector.memset(scale_table[:].bitcast(I32), 0)
        x_plane = keep.tile([P, S], U8, name="x_plane", align_bytes=64)
        nc.vector.memset(x_plane[:].bitcast(I32), 0)

        warm_in = keep.tile([P, 1], F32, name="warm_in")
        warm_out = keep.tile([P, 1], F32, name="warm_out")
        nc.vector.memset(warm_in[:], 0.0)
        nc.scalar.activation(warm_out[:], warm_in[:], SIGMOID)

        w1_raw = keep.tile([P, PACK, N], F32, name="w1_raw")
        w1_rows = w1.rearrange("(p j) c -> p j c", j=PACK)
        nc.sync.dma_start(w1_raw[:, 0:2, :], w1_rows[:, 0:2, :])
        nc.sync.dma_start(scale_table[0:P:8, :].bitcast(I32), x_scales[0].bitcast(I32))
        nc.sync.dma_start(w1_raw[:, 2:4, :], w1_rows[:, 2:4, :])
        word_table = keep.tile([P, T], I32, name="word_table", align_bytes=64)
        nc.sync.dma_start(word_table[:], x_words[0].rearrange("p n t -> p (n t)").bitcast(I32))
        w2_rows = w2.rearrange("(p j) c -> p j c", j=PACK)
        w2_raw = [keep.tile([P, PACK, HALF], F32, name="w2_raw%d" % h) for h in range(2)]
        nc.sync.dma_start(w2_raw[0][:], w2_rows[:, :, 0:HALF])

        picked_scales = keep.tile([P, S], U8, name="picked_scales", align_bytes=64)
        nc.vector.tensor_copy(picked_scales[:], scale_table[:].indirect(offsets[:]))
        for r in range(4):
            nc.sync.dma_start(x_plane[r:P:32, :].bitcast(I32), picked_scales[8 * r : P : 32, :].bitcast(I32))

        nc.sync.dma_start(w2_raw[1][:], w2_rows[:, :, HALF:N])
        hid_rows = hid.rearrange("(p t) j -> p t j", t=PACK)
        hid_half = []
        for h in range(2):
            part = keep.tile([P, PACK, HALF], F32, name="hid%d" % h)
            nc.sync.dma_start(part[:], hid_rows[:, :, h * HALF : (h + 1) * HALF])
            hid_half.append(part)

        def deal(engine_copy, grouped, raw, m0, lo, hi):
            engine_copy(
                grouped[:].rearrange("p (u v m j) -> p u m j v", u=2, v=2, j=PACK)[:, :, lo:hi],
                raw[:].rearrange("p j (m u v) -> p u m j v", u=2, v=2)[:, :, lo - m0 : hi - m0],
            )

        def quantize(grouped, label):
            codes = keep.tile([P, N], U32, name=label + "_codes", align_bytes=64)
            plane = keep.tile([P, N], U8, name=label + "_plane", align_bytes=64)
            nc.vector.quantize_mx(out=codes[:].bitcast(FP8X4), scales=plane[:], in_=grouped[:])
            return codes, plane

        w1_grouped = keep.tile([P, PACK * N], BF16, name="w1_grouped", align_bytes=64)
        deal(nc.scalar.copy, w1_grouped, w1_raw, 0, 0, 44)
        deal(nc.vector.tensor_copy, w1_grouped, w1_raw, 0, 44, P)
        w1_codes, w1_plane = quantize(w1_grouped, "w1")

        x_codes = keep.tile([P, S], U32, name="x_codes", align_bytes=64)
        nc.vector.tensor_copy(x_codes[:], word_table[:].bitcast(U32).indirect(offsets[:]))

        def product(codes, plane, c, label):
            bank = psum.tile([P, PACK, CHUNK], F32, name="%s%d" % (label, c))
            cols = slice(c * CHUNK, (c + 1) * CHUNK)
            for t in range(PACK):
                nc.tensor.matmul_mx(
                    out=bank[:, t, :],
                    lhsT=codes[:, t * P : (t + 1) * P].bitcast(FP8X4),
                    lhsT_scale=plane[:, t * P : (t + 1) * P],
                    rhs=x_codes[:, cols].bitcast(FP8X4),
                    rhs_scale=x_plane[:, cols],
                    start=True,
                    stop=True,
                )
            return bank

        keys = [product(w1_codes, w1_plane, c, "key") for c in range(CHUNKS)]

        out_rows = out_0.rearrange("(p t) j -> p t j", t=PACK)
        y_codes = keep.tile([P, S], U32, name="y_codes", align_bytes=64)
        y_plane = keep.tile([P, S], U8, name="y_plane", align_bytes=64)
        out_words = out_1[0].rearrange("p n t -> p (n t)").bitcast(I32)

        def hid_chunk(c):
            lo = (c * CHUNK) % HALF
            return hid_half[c * CHUNK // HALF][:, :, lo : lo + CHUNK]

        gates, gated, results = {}, {}, {}
        grouped = [keep.tile([P, PACK * HALF], BF16, name="y_grouped%d" % h, align_bytes=64) for h in range(2)]

        def gate(c):
            logits = keep.tile([P, PACK, CHUNK], F32, name="logits%d" % c)
            nc.vector.tensor_tensor(logits[:], hid_chunk(c), keys[c][:], MULT)
            gates[c] = keep.tile([P, PACK, CHUNK], F32, name="gate%d" % c)
            nc.scalar.activation(gates[c][:], logits[:], SIGMOID)

        def weigh(c):
            gated[c] = keep.tile([P, PACK, CHUNK], F32, name="gated%d" % c)
            nc.vector.tensor_tensor(gated[c][:], gates[c][:], vals[c][:], MULT)

        middle = keep.tile([P, PACK, HALF], F32, name="result12")
        results[0] = keep.tile([P, PACK, CHUNK], F32, name="result0")[:]
        results[1] = middle[:, :, 0:CHUNK]
        results[2] = middle[:, :, CHUNK:HALF]
        results[3] = keep.tile([P, PACK, CHUNK], F32, name="result3")[:]

        def finish(c, adder):
            adder(results[c], hid_chunk(c), gated[c][:], ADD)
            if c == 2:
                nc.sync.dma_start(out_rows[:, :, CHUNK : 3 * CHUNK], middle[:])
            elif c != 1:
                nc.sync.dma_start(out_rows[:, :, c * CHUNK : (c + 1) * CHUNK], results[c])

        def weave(c, rounder, lo, hi):
            base = (c * CHUNK) % HALF
            rounder(
                grouped[c * CHUNK // HALF][:, PACK * (base + lo) : PACK * (base + hi)].rearrange(
                    "p (c i t) -> p c t i", i=4, t=PACK
                ),
                results[c][:, :, lo:hi].rearrange("p t (c i) -> p c t i", i=4),
            )

        def pack(lo, hi):
            base = lo % HALF
            nc.vector.quantize_mx(
                out=y_codes[:, lo:hi].bitcast(FP8X4),
                scales=y_plane[:, lo:hi],
                in_=grouped[lo // HALF][:, PACK * base : PACK * (base + hi - lo)],
            )

        w2_grouped = keep.tile([P, PACK * N], BF16, name="w2_grouped", align_bytes=64)
        deal(nc.scalar.copy, w2_grouped, w2_raw[0], 0, 0, 32)
        deal(nc.vector.tensor_copy, w2_grouped, w2_raw[0], 0, 32, 64)
        deal(nc.scalar.copy, w2_grouped, w2_raw[1], 64, 64, 84)
        deal(nc.vector.tensor_copy, w2_grouped, w2_raw[1], 64, 84, P)
        w2_codes, w2_plane = quantize(w2_grouped, "w2")
        vals = [product(w2_codes, w2_plane, c, "val") for c in range(CHUNKS)]

        gate(0)
        gate(1)
        weigh(0)
        finish(0, nc.gpsimd.tensor_tensor)
        gate(2)
        gate(3)
        weigh(1)
        finish(1, nc.gpsimd.tensor_tensor)
        weave(0, nc.scalar.copy, 0, CHUNK)
        weigh(2)
        weave(1, nc.scalar.copy, 0, CHUNK)
        weigh(3)
        finish(2, nc.vector.tensor_tensor)
        weave(2, nc.scalar.copy, 0, CHUNK)
        finish(3, nc.vector.tensor_tensor)
        weave(3, nc.scalar.copy, 0, 48)
        pack(0, HALF)
        nc.sync.dma_start(out_words[:, 0:HALF], y_codes[:, 0:HALF].bitcast(I32))
        weave(3, nc.vector.tensor_copy, 48, CHUNK)
        pack(2 * CHUNK, 3 * CHUNK)
        pack(3 * CHUNK, S)
        nc.sync.dma_start(out_words[:, HALF:S], y_codes[:, HALF:S].bitcast(I32))
        for q in range(4):
            queue = nc.scalar if q % 2 == 0 else nc.sync
            queue.dma_start(out_2[0, 4 * q : 4 * q + 4, :].bitcast(I32), y_plane[32 * q : 32 * q + 4, :].bitcast(I32))
